import numpy as np
import ml_dtypes


def mxq(x, axis, fmt="e4m3"):
    dtype, down = {"e4m3": (ml_dtypes.float8_e4m3fn, 7), "e5m2": (ml_dtypes.float8_e5m2, 14)}[fmt]
    v = np.moveaxis(np.asarray(x, np.float32).astype(ml_dtypes.bfloat16).astype(np.float64), axis, -1)
    blocks = v.reshape(v.shape[:-1] + (-1, 32))
    amax = np.abs(blocks).max(-1, keepdims=True)
    byte = np.maximum(np.where(amax > 0, np.frexp(amax)[1] - 1 + 127, 0) - down, 1)
    scale = np.exp2(byte - 127.0)
    codes = (blocks / scale).astype(np.float32).astype(dtype).astype(np.float64)
    return np.moveaxis((codes * scale).reshape(v.shape), -1, axis)


WIDE = False


def mx_kscale(k):
    if not WIDE:
        return np.ones(k)
    levels = np.array([24, -24, 12, -12, 0])
    if k % 512:
        return np.exp2(np.random.permutation(np.resize(levels, k // 32))).repeat(32)
    a = np.empty((k // 512, 16))
    for p in range(k // 512):
        a[p, :8] = np.random.permutation(np.resize(levels, 8))
        for g in range(8):
            far = levels[np.abs(levels - a[p, g]) >= 10]
            a[p, g + 8] = far[np.random.randint(len(far))]
    return np.exp2(a.ravel()).repeat(32)


def f64(x):
    return np.asarray(x).astype(np.float64)


E2M1 = np.array([0.0, 0.5, 1.0, 1.5, 2.0, 3.0, 4.0, 6.0, -0.0, -0.5, -1.0, -1.5, -2.0, -3.0, -4.0, -6.0])


def pack_weight(w, fmt):
    k, n = w.shape
    w = f64(np.asarray(w, np.float32).astype(ml_dtypes.bfloat16)).reshape(k // 32, 32, n)
    amax = np.abs(w).max(1)
    if fmt == "e4m3":
        byte = np.frexp(amax)[1] - 1 + 127 - 7
    else:
        mant, ex = np.frexp(amax / 6.0)
        byte = np.where(mant > 0.5, ex, ex - 1) + 127
    byte = np.clip(np.where(amax > 0, byte, 1), 1, 254)
    scaled = (w * np.exp2(127.0 - byte)[:, None, :]).reshape(k, n).astype(np.float32)
    by_word = np.ascontiguousarray(scaled.reshape(k // 512, 128, 4, n).transpose(0, 1, 3, 2))
    if fmt == "e4m3":
        words = by_word.astype(ml_dtypes.float8_e4m3fn).view(np.uint8)
    else:
        c = by_word.astype(ml_dtypes.float4_e2m1fn).view(np.uint8) & 0xF
        words = (c[..., 0::2] | (c[..., 1::2] << 4)).reshape(k // 512, 128, 2 * n)
    return np.ascontiguousarray(words), np.ascontiguousarray(byte.astype(np.uint8).reshape(k // 512, 16, n))


def unpack_weight(words, scales, fmt):
    g, _, n = scales.shape
    words = np.ascontiguousarray(words).reshape(g, 128, n, -1)
    if fmt == "e4m3":
        vals = words.view(ml_dtypes.float8_e4m3fn).astype(np.float64)
    else:
        nib = np.empty((g, 128, n, 4), np.uint8)
        nib[..., 0::2] = words & 0xF
        nib[..., 1::2] = words >> 4
        vals = E2M1[nib]
    vals = vals * np.repeat(np.exp2(scales.astype(np.float64) - 127.0), 8, axis=1)[..., None]
    return vals.transpose(0, 1, 3, 2).reshape(g * 512, n)


def planes(y):
    n, m = y.shape
    v = y.astype(np.float32).astype(ml_dtypes.bfloat16).astype(np.float64).reshape(n // 32, 32, m)
    top = np.abs(v).max(1)
    byte = np.clip(np.where(top > 0, np.frexp(top)[1] - 1 + 127 - 7, 1), 1, 254)
    codes = (v * np.exp2(127.0 - byte)[:, None, :]).reshape(n, m).astype(np.float32).astype(ml_dtypes.float8_e4m3fn).view(np.uint8)
    words = codes.reshape(n // 512, 128, 4, m).transpose(0, 1, 3, 2)
    return np.ascontiguousarray(words), np.ascontiguousarray(byte.astype(np.uint8).reshape(n // 512, 16, m))


def sigm(f):
    return 1.0 / (1.0 + np.exp(-np.maximum(f, -700.0)))


K, N, T, M = 512, 512, 1024, 512


def setup_inputs():
    n = np.random.standard_normal
    s = mx_kscale(K)[:, None]
    s2 = mx_kscale(N)[:, None]
    h = np.tanh(n((N, T)))
    p_hq = pack_weight(h * s2, "e4m3")
    p_wz = pack_weight(n((K, N)) / np.sqrt(K) / s, "e2m1")
    p_uz = pack_weight(n((N, N)) / np.sqrt(N) / s2, "e2m1")
    p_wn = pack_weight(n((K, N)) / np.sqrt(K) / s, "e2m1")
    p_un = pack_weight(n((N, N)) / np.sqrt(N) / s2, "e2m1")
    return {
        "x": (n((K, T)) * s).astype(np.float32),
        "hq_words": p_hq[0],
        "hq_scales": p_hq[1],
        "wz_words": p_wz[0],
        "wz_scales": p_wz[1],
        "uz_words": p_uz[0],
        "uz_scales": p_uz[1],
        "wn_words": p_wn[0],
        "wn_scales": p_wn[1],
        "un_words": p_un[0],
        "un_scales": p_un[1],
        "bz": (0.3 * n(N)).astype(np.float32),
        "bn": (0.3 * n(N)).astype(np.float32),
        "h": (h).astype(np.float32),
    }


def reference(x, hq_words, hq_scales, wz_words, wz_scales, uz_words, uz_scales, wn_words, wn_scales, un_words, un_scales, bz, bn, h):
    x_ = mxq(f64(x), 0, "e4m3")
    hq_ = unpack_weight(hq_words, hq_scales, "e4m3")
    wz_ = unpack_weight(wz_words, wz_scales, "e2m1")
    uz_ = unpack_weight(uz_words, uz_scales, "e2m1")
    wn_ = unpack_weight(wn_words, wn_scales, "e2m1")
    un_ = unpack_weight(un_words, un_scales, "e2m1")
    sz = wz_.T @ x_ + uz_.T @ hq_
    z = sigm(sz + f64(bz)[:, None])
    xn = wn_.T @ x_
    hn = un_.T @ hq_
    c = np.tanh(xn + f64(bn)[:, None] + z * hn)
    out_0 = f64(h) + z * (c - f64(h))
    return (out_0,) + planes(out_0)

@@ -1,0 +1,267 @@
+from contextlib import ExitStack
+
+import concourse.mybir as mybir
+
+K, N, T = 512, 512, 1024
+FLOPS = 4 * 2 * K * N * T
+
+F32 = mybir.dt.float32
+BF16 = mybir.dt.bfloat16
+I32 = mybir.dt.int32
+U32 = mybir.dt.uint32
+U8 = mybir.dt.uint8
+FP8X4 = mybir.dt.float8_e4m3fn_x4
+FP4X4 = mybir.dt.float4_e2m1fn_x4
+ALU = mybir.AluOpType
+ACT = mybir.ActivationFunctionType
+
+P = 128
+PACK = 4
+W = 128
+UNITS = T // W
+WZ, UZ, UN, WN = 0, 1, 2, 3
+POOL_UNITS = (0, 1, 2, 3, 4, 5)
+X_LOADS = [(0, 1), (1, 2), (2, 4), (4, 8)]
+H_LOADS = [(0, 2), (2, 4), (4, 8)]
+HQ_LOADS = [(0, 2), (2, 8)]
+OUT_STORES = [(0, 2), (2, 4), (4, 6), (6, 7), (7, 8)]
+CODE_STORES = [(0, 4), (4, 6), (6, 8)]
+
+
+def find(ranges, u):
+    for lo, hi in ranges:
+        if lo <= u < hi:
+            return lo, hi
+    raise ValueError("unit outside the ranges")
+
+
+def tile_mix_gru_mgu_kernel(
+    tc, x, hq_words, hq_scales, wz_words, wz_scales, uz_words, uz_scales,
+    wn_words, wn_scales, un_words, un_scales, bz, bn, h, out_0, out_1, out_2,
+):
+    nc = tc.nc
+    w_words = [wz_words, uz_words, un_words, wn_words]
+    w_scales = [wz_scales, uz_scales, un_scales, wn_scales]
+    x_rows = x.rearrange("(p j) t -> p j t", j=PACK)
+    h_rows = h.rearrange("(p j) t -> p j t", j=PACK)
+    out_rows = out_0.rearrange("(p j) t -> p j t", j=PACK)
+    hq_flat = hq_words[0].rearrange("p t i -> p (t i)").bitcast(I32)
+    codes_flat = out_1[0].rearrange("p t i -> p (t i)").bitcast(I32)
+    scales_flat = out_2[0].bitcast(I32)
+
+    with ExitStack() as ctx:
+        keep = ctx.enter_context(tc.tile_pool(name="keep", bufs=1))
+        work = ctx.enter_context(tc.tile_pool(name="work", bufs=UNITS))
+        psum = ctx.enter_context(tc.psum_pool(name="psum", bufs=1))
+        ctx.enter_context(tc.manual_schedule())
+
+        stage = keep.tile([16, (4 * N + T) // 4], I32, name="stage")
+        planes = keep.tile([P, 4 * N + T], U8, name="planes", align_bytes=64)
+        w_plane = keep.tile([P, 4 * N], U8, name="w_plane", align_bytes=64)
+        w_raw = [keep.tile([P, 2 * N], U8, name="w_raw%d" % w, align_bytes=64) for w in range(4)]
+        w_code = [keep.tile([P, 2 * N], U8, name="w_code%d" % w, align_bytes=64) for w in range(4)]
+        x_sb = {r: keep.tile([P, PACK, (r[1] - r[0]) * W], F32, name="x%d" % r[0], align_bytes=64) for r in X_LOADS}
+        h_sb = {r: keep.tile([P, PACK, (r[1] - r[0]) * W], F32, name="h%d" % r[0], align_bytes=64) for r in H_LOADS}
+        hq_sb = {r: keep.tile([P, (r[1] - r[0]) * W], I32, name="hq%d" % r[0], align_bytes=64) for r in HQ_LOADS}
+        o_sb = {r: keep.tile([P, PACK, (r[1] - r[0]) * W], F32, name="o%d" % r[0], align_bytes=64) for r in OUT_STORES}
+        x_code = keep.tile([P, T], U32, name="x_code", align_bytes=64)
+        x_plane = keep.tile([P, T], U8, name="x_plane", align_bytes=64)
+        o_code = keep.tile([P, T], U32, name="o_code", align_bytes=64)
+        o_plane = keep.tile([P, T], U8, name="o_plane", align_bytes=64)
+        bz_sb = keep.tile([P, PACK], F32, name="bz_sb")
+        bz_half = keep.tile([P, PACK], F32, name="bz_half")
+        bn_sb = keep.tile([P, PACK], F32, name="bn_sb")
+
+        tiles = {}
+
+        def cols(u):
+            return slice(u * W, (u + 1) * W)
+
+        def unit_of(sb, ranges, u):
+            lo, hi = find(ranges, u)
+            return sb[(lo, hi)][:, :, cols(u - lo)]
+
+        def load_rows(sb, rows, r):
+            nc.sync.dma_start(out=sb[r][:], in_=rows[:, :, r[0] * W : r[1] * W])
+
+        def load_hq(r):
+            nc.sync.dma_start(out=hq_sb[r][:], in_=hq_flat[:, r[0] * W : r[1] * W])
+
+        def load_words(w):
+            nc.sync.dma_start(out=w_raw[w][:].bitcast(I32), in_=w_words[w][0].bitcast(I32))
+
+        def deal_words(w):
+            nc.vector.tensor_copy(
+                out=w_code[w][:].rearrange("p (r m b) -> p r m b", r=PACK, b=2),
+                in_=w_raw[w][:].rearrange("p (m r b) -> p r m b", r=PACK, b=2),
+            )
+
+        def deal_scales(lo, hi):
+            nc.vector.tensor_copy(
+                out=w_plane[:, lo * N : hi * N].rearrange("p (w r m) -> p w r m", r=PACK, m=P),
+                in_=planes[:, lo * N : hi * N].rearrange("p (w m r) -> p w r m", r=PACK, m=P),
+            )
+
+        def interleave(engine, key, src):
+            dst = work.tile([P, W * PACK], BF16, name=key[0], align_bytes=64)
+            tiles[key] = dst
+            out = dst[:].rearrange("p (c i j) -> p c j i", i=4, j=PACK)
+            in_ = src.rearrange("p j (c i) -> p c j i", i=4)
+            if engine == "scalar":
+                nc.scalar.activation(out=out, in_=in_, func=ACT.Copy)
+            else:
+                nc.vector.tensor_copy(out=out, in_=in_)
+
+        def round_x(u, engine="scalar"):
+            interleave(engine, ("xb", u), unit_of(x_sb, X_LOADS, u))
+
+        def round_out(u, engine="scalar"):
+            interleave(engine, ("ob", u), unit_of(o_sb, OUT_STORES, u))
+
+        def quantize_x(u):
+            nc.vector.quantize_mx(out=x_code[:, cols(u)].bitcast(FP8X4), scales=x_plane[:, cols(u)], in_=tiles[("xb", u)][:])
+
+        def quantize_out(u):
+            nc.vector.quantize_mx(out=o_code[:, cols(u)].bitcast(FP8X4), scales=o_plane[:, cols(u)], in_=tiles[("ob", u)][:])
+
+        def product(key, u, weights, bufs):
+            acc = psum.tile([P, PACK, W], F32, name=key, bufs=bufs)
+            tiles[(key, u)] = acc
+            lo, hi = find(HQ_LOADS, u)
+            for r in range(PACK):
+                for n, w in enumerate(weights):
+                    if w in (WZ, WN):
+                        rhs, rhs_scale = x_code[:, cols(u)], x_plane[:, cols(u)]
+                    else:
+                        rhs = hq_sb[(lo, hi)][:, cols(u - lo)]
+                        rhs_scale = planes[:, 4 * N + u * W : 4 * N + (u + 1) * W]
+                    nc.tensor.matmul_mx(
+                        out=acc[:, r, :],
+                        lhsT=w_code[w][:, r * 2 * P : (r + 1) * 2 * P].bitcast(FP4X4),
+                        lhsT_scale=w_plane[:, w * N + r * P : w * N + (r + 1) * P],
+                        rhs=rhs.bitcast(FP8X4),
+                        rhs_scale=rhs_scale,
+                        start=(n == 0),
+                        stop=(n == len(weights) - 1),
+                    )
+
+        def fresh(key, u, bufs=None):
+            if bufs is None:
+                t = work.tile([P, PACK, W], F32, name=key, align_bytes=64)
+            else:
+                t = work.tile([P, PACK, W], F32, name=key, align_bytes=64, bufs=bufs)
+            tiles[(key, u)] = t
+            return t
+
+        def gate(u):
+            g = fresh("g", u)
+            for r in range(PACK):
+                nc.scalar.activation(out=g[:, r, :], in_=tiles[("sz", u)][:, r, :], func=ACT.Tanh, bias=bz_half[:, r : r + 1], scale=0.5)
+
+        def gated_state(u):
+            nc.vector.scalar_tensor_tensor(out=fresh("zh", u)[:], in0=tiles[("g", u)][:], scalar=1.0, in1=tiles[("hn", u)][:], op0=ALU.add, op1=ALU.mult)
+
+        def pre_activation(u):
+            nc.vector.scalar_tensor_tensor(out=fresh("pre", u)[:], in0=tiles[("zh", u)][:], scalar=0.5, in1=tiles[("xn", u)][:], op0=ALU.mult, op1=ALU.add)
+
+        def candidate(u):
+            c = fresh("c", u)
+            for r in range(PACK):
+                nc.scalar.activation(out=c[:, r, :], in_=tiles[("pre", u)][:, r, :], func=ACT.Tanh, bias=bn_sb[:, r : r + 1])
+
+        def difference(u):
+            if u in POOL_UNITS:
+                d = fresh("dp", u, bufs=1)
+                nc.gpsimd.tensor_tensor(out=d[:], in0=tiles[("c", u)][:], in1=unit_of(h_sb, H_LOADS, u), op=ALU.subtract)
+            else:
+                d = fresh("dv", u)
+                nc.vector.tensor_tensor(out=d[:], in0=tiles[("c", u)][:], in1=unit_of(h_sb, H_LOADS, u), op=ALU.subtract)
+            tiles[("d", u)] = d
+
+        def step(u):
+            nc.vector.scalar_tensor_tensor(out=fresh("e", u)[:], in0=tiles[("g", u)][:], scalar=1.0, in1=tiles[("d", u)][:], op0=ALU.add, op1=ALU.mult)
+
+        def new_state(u):
+            nc.vector.scalar_tensor_tensor(out=unit_of(o_sb, OUT_STORES, u), in0=tiles[("e", u)][:], scalar=0.5, in1=unit_of(h_sb, H_LOADS, u), op0=ALU.mult, op1=ALU.add)
+            lo, hi = find(OUT_STORES, u)
+            if u == hi - 1:
+                nc.sync.dma_start(out=out_rows[:, :, lo * W : hi * W], in_=o_sb[(lo, hi)][:])
+
+        def hand_on(u):
+            quantize_out(u)
+            lo, hi = find(CODE_STORES, u)
+            if u == hi - 1:
+                nc.sync.dma_start(out=codes_flat[:, lo * W : hi * W], in_=o_code[:, lo * W : hi * W].bitcast(I32))
+
+        def live(u):
+            return 0 <= u < UNITS
+
+        nc.vector.memset(planes[:].bitcast(I32), 0)
+        nc.gpsimd.dma_start(out=bz_sb[:], in_=bz.rearrange("(p j) -> p j", j=PACK))
+        nc.gpsimd.dma_start(out=bn_sb[:], in_=bn.rearrange("(p j) -> p j", j=PACK))
+        nc.gpsimd.tensor_scalar(out=bz_half[:], in0=bz_sb[:], scalar1=0.5, scalar2=0.0, op0=ALU.mult, op1=ALU.add)
+        for w in range(4):
+            nc.sync.dma_start(out=stage[:, w * N // 4 : (w + 1) * N // 4], in_=w_scales[w][0].bitcast(I32))
+        nc.sync.dma_start(out=stage[:, N:], in_=hq_scales[0].bitcast(I32))
+        load_words(WZ)
+        load_words(UZ)
+        load_rows(x_sb, x_rows, X_LOADS[0])
+        for r in range(4):
+            nc.sync.dma_start(out=planes[r:P:32, :].bitcast(I32), in_=stage[r:16:4, :])
+        load_words(UN)
+        load_hq(HQ_LOADS[0])
+        load_words(WN)
+        load_rows(x_sb, x_rows, X_LOADS[1])
+        load_rows(x_sb, x_rows, X_LOADS[2])
+        load_rows(h_sb, h_rows, H_LOADS[0])
+        load_hq(HQ_LOADS[1])
+        load_rows(x_sb, x_rows, X_LOADS[3])
+        load_rows(h_sb, h_rows, H_LOADS[1])
+        load_rows(h_sb, h_rows, H_LOADS[2])
+
+        round_x(0)
+        round_x(1)
+        deal_words(WZ)
+        deal_words(UZ)
+        quantize_x(0)
+        deal_words(UN)
+        deal_scales(WZ, UN + 1)
+        product("sz", 0, [WZ, UZ], 2)
+        product("hn", 0, [UN], 3)
+        gate(0)
+        round_x(2)
+        quantize_x(1)
+        deal_words(WN)
+        deal_scales(WN, WN + 1)
+
+        for i in range(UNITS + 4):
+            if live(i + 1):
+                product("sz", i + 1, [WZ, UZ], 2)
+            if live(i):
+                product("xn", i, [WN], 3)
+            if live(i + 1):
+                product("hn", i + 1, [UN], 3)
+            if live(i - 4):
+                round_out(i - 4, "vector" if i - 4 == UNITS - 1 else "scalar")
+            if live(i + 1):
+                gate(i + 1)
+            if live(i - 2):
+                difference(i - 2)
+            if live(i):
+                gated_state(i)
+            if live(i - 1):
+                pre_activation(i - 1)
+                candidate(i - 1)
+            if live(i + 3):
+                round_x(i + 3)
+            if live(i + 2):
+                quantize_x(i + 2)
+            if live(i - 4):
+                hand_on(i - 4)
+            if live(i - 2):
+                step(i - 2)
+            if live(i - 3):
+                new_state(i - 3)
+
+        for q in range(4):
+            nc.sync.dma_start(out=scales_flat[4 * q : 4 * q + 4, :], in_=o_plane[32 * q : 32 * q + 4, :].bitcast(I32))

@@ -17,22 +17,25 @@ ACT = mybir.ActivationFunctionType
 
 P = 128
 PACK = 4
-W = 128
-UNITS = T // W
+BANK = 512
+SUM_N = 128
 WZ, UZ, UN, WN = 0, 1, 2, 3
-POOL_UNITS = (0, 1, 2, 3, 4, 5)
-X_LOADS = [(0, 1), (1, 2), (2, 4), (4, 8)]
-H_LOADS = [(0, 2), (2, 4), (4, 8)]
-HQ_LOADS = [(0, 2), (2, 8)]
-OUT_STORES = [(0, 2), (2, 4), (4, 6), (6, 7), (7, 8)]
-CODE_STORES = [(0, 4), (4, 6), (6, 8)]
+WIDTHS = [128] * 8
+STARTS = [sum(WIDTHS[:c]) for c in range(len(WIDTHS) + 1)]
+UNITS = [(c, r0, BANK // w) for c, w in enumerate(WIDTHS) for r0 in range(0, PACK, BANK // w)]
+POOL_UNITS = tuple(range(8))
+X_LOADS = [(0, 2), (2, 3), (3, 5), (5, 8)]
+H_LOADS = [(0, 1), (1, 3), (3, 5), (5, 8)]
+HQ_LOADS = [(0, 3), (3, 8)]
+CODE_STORES = [(0, 4), (4, 7), (7, 8)]
+KEPT_BUFS = 4
 
 
-def find(ranges, u):
+def find(ranges, c):
     for lo, hi in ranges:
-        if lo <= u < hi:
+        if lo <= c < hi:
             return lo, hi
-    raise ValueError("unit outside the ranges")
+    raise ValueError("chunk outside the ranges")
 
 
 def tile_mix_gru_mgu_kernel(
@@ -51,44 +54,57 @@ def tile_mix_gru_mgu_kernel(
 
     with ExitStack() as ctx:
         keep = ctx.enter_context(tc.tile_pool(name="keep", bufs=1))
-        work = ctx.enter_context(tc.tile_pool(name="work", bufs=UNITS))
+        work = ctx.enter_context(tc.tile_pool(name="work", bufs=len(UNITS)))
         psum = ctx.enter_context(tc.psum_pool(name="psum", bufs=1))
         ctx.enter_context(tc.manual_schedule())
+
+        def span(r):
+            return slice(STARTS[r[0]], STARTS[r[1]])
+
+        def width(r):
+            return STARTS[r[1]] - STARTS[r[0]]
+
+        def cols(c):
+            return span((c, c + 1))
 
         stage = keep.tile([16, (4 * N + T) // 4], I32, name="stage")
         planes = keep.tile([P, 4 * N + T], U8, name="planes", align_bytes=64)
         w_plane = keep.tile([P, 4 * N], U8, name="w_plane", align_bytes=64)
         w_raw = [keep.tile([P, 2 * N], U8, name="w_raw%d" % w, align_bytes=64) for w in range(4)]
         w_code = [keep.tile([P, 2 * N], U8, name="w_code%d" % w, align_bytes=64) for w in range(4)]
-        x_sb = {r: keep.tile([P, PACK, (r[1] - r[0]) * W], F32, name="x%d" % r[0], align_bytes=64) for r in X_LOADS}
-        h_sb = {r: keep.tile([P, PACK, (r[1] - r[0]) * W], F32, name="h%d" % r[0], align_bytes=64) for r in H_LOADS}
-        hq_sb = {r: keep.tile([P, (r[1] - r[0]) * W], I32, name="hq%d" % r[0], align_bytes=64) for r in HQ_LOADS}
-        o_sb = {r: keep.tile([P, PACK, (r[1] - r[0]) * W], F32, name="o%d" % r[0], align_bytes=64) for r in OUT_STORES}
+        x_sb = {r: keep.tile([P, PACK, width(r)], F32, name="x%d" % r[0], align_bytes=64) for r in X_LOADS}
+        h_sb = {r: keep.tile([P, PACK, width(r)], F32, name="h%d" % r[0], align_bytes=64) for r in H_LOADS}
+        hq_sb = {r: keep.tile([P, width(r)], I32, name="hq%d" % r[0], align_bytes=64) for r in HQ_LOADS}
+        o_sb = [keep.tile([P, PACK, w], F32, name="o%d" % c, align_bytes=64) for c, w in enumerate(WIDTHS)]
+        x_bf = [keep.tile([P, PACK * w], BF16, name="xb%d" % c, align_bytes=64) for c, w in enumerate(WIDTHS)]
+        o_bf = [keep.tile([P, PACK * w], BF16, name="ob%d" % c, align_bytes=64) for c, w in enumerate(WIDTHS)]
         x_code = keep.tile([P, T], U32, name="x_code", align_bytes=64)
         x_plane = keep.tile([P, T], U8, name="x_plane", align_bytes=64)
         o_code = keep.tile([P, T], U32, name="o_code", align_bytes=64)
         o_plane = keep.tile([P, T], U8, name="o_plane", align_bytes=64)
         bz_sb = keep.tile([P, PACK], F32, name="bz_sb")
-        bz_half = keep.tile([P, PACK], F32, name="bz_half")
+        bz_neg = keep.tile([P, PACK], F32, name="bz_neg")
         bn_sb = keep.tile([P, PACK], F32, name="bn_sb")
 
         tiles = {}
 
-        def cols(u):
-            return slice(u * W, (u + 1) * W)
+        def chunk_of(sb, ranges, c):
+            r = find(ranges, c)
+            return slice(STARTS[c] - STARTS[r[0]], STARTS[c + 1] - STARTS[r[0]]), sb[r]
 
-        def unit_of(sb, ranges, u):
-            lo, hi = find(ranges, u)
-            return sb[(lo, hi)][:, :, cols(u - lo)]
+        def h_of(u):
+            c, r0, rows = UNITS[u]
+            part, tile = chunk_of(h_sb, H_LOADS, c)
+            return tile[:, r0 : r0 + rows, part]
 
-        def load_rows(sb, rows, r):
-            nc.sync.dma_start(out=sb[r][:], in_=rows[:, :, r[0] * W : r[1] * W])
+        def load_rows(sb, rows, r, queue=nc.sync):
+            queue.dma_start(out=sb[r][:], in_=rows[:, :, span(r)])
 
         def load_hq(r):
-            nc.sync.dma_start(out=hq_sb[r][:], in_=hq_flat[:, r[0] * W : r[1] * W])
+            nc.sync.dma_start(out=hq_sb[r][:], in_=hq_flat[:, span(r)])
 
-        def load_words(w):
-            nc.sync.dma_start(out=w_raw[w][:].bitcast(I32), in_=w_words[w][0].bitcast(I32))
+        def load_words(w, queue=nc.sync):
+            queue.dma_start(out=w_raw[w][:].bitcast(I32), in_=w_words[w][0].bitcast(I32))
 
         def deal_words(w):
             nc.vector.tensor_copy(
@@ -96,128 +112,133 @@ def tile_mix_gru_mgu_kernel(
                 in_=w_raw[w][:].rearrange("p (m r b) -> p r m b", r=PACK, b=2),
             )
 
-        def deal_scales(lo, hi):
+        def deal_scales(lo, hi, r0=0, r1=PACK):
             nc.vector.tensor_copy(
-                out=w_plane[:, lo * N : hi * N].rearrange("p (w r m) -> p w r m", r=PACK, m=P),
-                in_=planes[:, lo * N : hi * N].rearrange("p (w m r) -> p w r m", r=PACK, m=P),
+                out=w_plane[:, lo * N : hi * N].rearrange("p (w r m) -> p w r m", r=PACK, m=P)[:, :, r0:r1, :],
+                in_=planes[:, lo * N : hi * N].rearrange("p (w m r) -> p w r m", r=PACK, m=P)[:, :, r0:r1, :],
             )
 
-        def interleave(engine, key, src):
-            dst = work.tile([P, W * PACK], BF16, name=key[0], align_bytes=64)
-            tiles[key] = dst
+        def interleave(engine, dst, src):
             out = dst[:].rearrange("p (c i j) -> p c j i", i=4, j=PACK)
             in_ = src.rearrange("p j (c i) -> p c j i", i=4)
             if engine == "scalar":
-                nc.scalar.activation(out=out, in_=in_, func=ACT.Copy)
+                nc.scalar.copy(out=out, in_=in_)
             else:
                 nc.vector.tensor_copy(out=out, in_=in_)
 
-        def round_x(u, engine="scalar"):
-            interleave(engine, ("xb", u), unit_of(x_sb, X_LOADS, u))
+        def round_x(c, engine="scalar"):
+            part, tile = chunk_of(x_sb, X_LOADS, c)
+            interleave(engine, x_bf[c], tile[:, :, part])
 
-        def round_out(u, engine="scalar"):
-            interleave(engine, ("ob", u), unit_of(o_sb, OUT_STORES, u))
+        def round_out(c, engine="scalar"):
+            interleave(engine, o_bf[c], o_sb[c][:])
 
-        def quantize_x(u):
-            nc.vector.quantize_mx(out=x_code[:, cols(u)].bitcast(FP8X4), scales=x_plane[:, cols(u)], in_=tiles[("xb", u)][:])
+        def quantize_x(c):
+            nc.vector.quantize_mx(out=x_code[:, cols(c)].bitcast(FP8X4), scales=x_plane[:, cols(c)], in_=x_bf[c][:])
 
-        def quantize_out(u):
-            nc.vector.quantize_mx(out=o_code[:, cols(u)].bitcast(FP8X4), scales=o_plane[:, cols(u)], in_=tiles[("ob", u)][:])
+        def hand_on(c):
+            nc.vector.quantize_mx(out=o_code[:, cols(c)].bitcast(FP8X4), scales=o_plane[:, cols(c)], in_=o_bf[c][:])
+            r = find(CODE_STORES, c)
+            if c == r[1] - 1:
+                nc.sync.dma_start(out=codes_flat[:, span(r)], in_=o_code[:, span(r)].bitcast(I32))
 
-        def product(key, u, weights, bufs):
-            acc = psum.tile([P, PACK, W], F32, name=key, bufs=bufs)
+        def product(key, u, weights, bufs, part=None):
+            c, r0, rows = UNITS[u]
+            if part is not None:
+                r0, rows = part
+            acc = psum.tile([P, rows, WIDTHS[c]], F32, name=key, bufs=bufs)
             tiles[(key, u)] = acc
-            lo, hi = find(HQ_LOADS, u)
-            for r in range(PACK):
-                for n, w in enumerate(weights):
-                    if w in (WZ, WN):
-                        rhs, rhs_scale = x_code[:, cols(u)], x_plane[:, cols(u)]
-                    else:
-                        rhs = hq_sb[(lo, hi)][:, cols(u - lo)]
-                        rhs_scale = planes[:, 4 * N + u * W : 4 * N + (u + 1) * W]
-                    nc.tensor.matmul_mx(
-                        out=acc[:, r, :],
-                        lhsT=w_code[w][:, r * 2 * P : (r + 1) * 2 * P].bitcast(FP4X4),
-                        lhsT_scale=w_plane[:, w * N + r * P : w * N + (r + 1) * P],
-                        rhs=rhs.bitcast(FP8X4),
-                        rhs_scale=rhs_scale,
-                        start=(n == 0),
-                        stop=(n == len(weights) - 1),
-                    )
+            part, hq_tile = chunk_of(hq_sb, HQ_LOADS, c)
+            hq_code = hq_tile[:, part]
+            hq_plane = planes[:, 4 * N + STARTS[c] : 4 * N + STARTS[c + 1]]
+            n_pass = WIDTHS[c] if len(weights) == 1 or WIDTHS[c] == BANK else SUM_N
+            for r in range(r0, r0 + rows):
+                for t0 in range(0, WIDTHS[c], n_pass):
+                    ts = slice(t0, t0 + n_pass)
+                    for n, w in enumerate(weights):
+                        code, plane = (x_code[:, cols(c)], x_plane[:, cols(c)]) if w in (WZ, WN) else (hq_code, hq_plane)
+                        nc.tensor.matmul_mx(
+                            out=acc[:, r - r0, ts],
+                            lhsT=w_code[w][:, r * 2 * P : (r + 1) * 2 * P].bitcast(FP4X4),
+                            lhsT_scale=w_plane[:, w * N + r * P : w * N + (r + 1) * P],
+                            rhs=code[:, ts].bitcast(FP8X4),
+                            rhs_scale=plane[:, ts],
+                            start=(n == 0),
+                            stop=(n == len(weights) - 1),
+                        )
 
-        def fresh(key, u, bufs=None):
-            if bufs is None:
-                t = work.tile([P, PACK, W], F32, name=key, align_bytes=64)
-            else:
-                t = work.tile([P, PACK, W], F32, name=key, align_bytes=64, bufs=bufs)
+        def fresh(key, u, bufs=len(UNITS)):
+            c, r0, rows = UNITS[u]
+            t = work.tile([P, rows, WIDTHS[c]], F32, name=key, align_bytes=64, bufs=bufs)
             tiles[(key, u)] = t
             return t
 
-        def gate(u):
-            g = fresh("g", u)
-            for r in range(PACK):
-                nc.scalar.activation(out=g[:, r, :], in_=tiles[("sz", u)][:, r, :], func=ACT.Tanh, bias=bz_half[:, r : r + 1], scale=0.5)
+        def gate(u, part=None):
+            c, r0, rows = UNITS[u]
+            if part is not None:
+                r0, rows = part
+            v = fresh("v", u) if ("v", u) not in tiles else tiles[("v", u)]
+            for r in range(rows):
+                nc.scalar.activation(out=v[:, r0 - UNITS[u][1] + r, :], in_=tiles[("sz", u)][:, r, :], func=ACT.Sigmoid, bias=bz_neg[:, r0 + r : r0 + r + 1], scale=-1.0)
+
+        def kept_state(u):
+            engine = nc.gpsimd if u in POOL_UNITS else nc.vector
+            engine.tensor_tensor(out=fresh("kept", u, KEPT_BUFS)[:], in0=tiles[("v", u)][:], in1=h_of(u), op=ALU.mult)
 
         def gated_state(u):
-            nc.vector.scalar_tensor_tensor(out=fresh("zh", u)[:], in0=tiles[("g", u)][:], scalar=1.0, in1=tiles[("hn", u)][:], op0=ALU.add, op1=ALU.mult)
+            nc.vector.scalar_tensor_tensor(out=fresh("zh", u)[:], in0=tiles[("v", u)][:], scalar=1.0, in1=tiles[("hn", u)][:], op0=ALU.subtract, op1=ALU.mult)
 
         def pre_activation(u):
-            nc.vector.scalar_tensor_tensor(out=fresh("pre", u)[:], in0=tiles[("zh", u)][:], scalar=0.5, in1=tiles[("xn", u)][:], op0=ALU.mult, op1=ALU.add)
+            nc.vector.tensor_tensor(out=fresh("pre", u)[:], in0=tiles[("xn", u)][:], in1=tiles[("zh", u)][:], op=ALU.subtract)
 
         def candidate(u):
-            c = fresh("c", u)
-            for r in range(PACK):
-                nc.scalar.activation(out=c[:, r, :], in_=tiles[("pre", u)][:, r, :], func=ACT.Tanh, bias=bn_sb[:, r : r + 1])
+            c, r0, rows = UNITS[u]
+            cand = fresh("cand", u)
+            for r in range(rows):
+                nc.scalar.activation(out=cand[:, r, :], in_=tiles[("pre", u)][:, r, :], func=ACT.Tanh, bias=bn_sb[:, r0 + r : r0 + r + 1])
 
-        def difference(u):
-            if u in POOL_UNITS:
-                d = fresh("dp", u, bufs=1)
-                nc.gpsimd.tensor_tensor(out=d[:], in0=tiles[("c", u)][:], in1=unit_of(h_sb, H_LOADS, u), op=ALU.subtract)
-            else:
-                d = fresh("dv", u)
-                nc.vector.tensor_tensor(out=d[:], in0=tiles[("c", u)][:], in1=unit_of(h_sb, H_LOADS, u), op=ALU.subtract)
-            tiles[("d", u)] = d
-
-        def step(u):
-            nc.vector.scalar_tensor_tensor(out=fresh("e", u)[:], in0=tiles[("g", u)][:], scalar=1.0, in1=tiles[("d", u)][:], op0=ALU.add, op1=ALU.mult)
+        def gated_candidate(u):
+            nc.vector.scalar_tensor_tensor(out=fresh("zc", u)[:], in0=tiles[("v", u)][:], scalar=1.0, in1=tiles[("cand", u)][:], op0=ALU.subtract, op1=ALU.mult)
 
         def new_state(u):
-            nc.vector.scalar_tensor_tensor(out=unit_of(o_sb, OUT_STORES, u), in0=tiles[("e", u)][:], scalar=0.5, in1=unit_of(h_sb, H_LOADS, u), op0=ALU.mult, op1=ALU.add)
-            lo, hi = find(OUT_STORES, u)
-            if u == hi - 1:
-                nc.sync.dma_start(out=out_rows[:, :, lo * W : hi * W], in_=o_sb[(lo, hi)][:])
-
-        def hand_on(u):
-            quantize_out(u)
-            lo, hi = find(CODE_STORES, u)
-            if u == hi - 1:
-                nc.sync.dma_start(out=codes_flat[:, lo * W : hi * W], in_=o_code[:, lo * W : hi * W].bitcast(I32))
+            c, r0, rows = UNITS[u]
+            nc.vector.tensor_tensor(out=o_sb[c][:, r0 : r0 + rows, :], in0=tiles[("kept", u)][:], in1=tiles[("zc", u)][:], op=ALU.subtract)
+            if r0 + rows == PACK:
+                nc.sync.dma_start(out=out_rows[:, :, cols(c)], in_=o_sb[c][:])
 
         def live(u):
-            return 0 <= u < UNITS
+            return 0 <= u < len(UNITS)
+
+        def opens(u):
+            return live(u) and UNITS[u][1] == 0
+
+        def closes(u):
+            return live(u) and UNITS[u][1] + UNITS[u][2] == PACK
 
         nc.vector.memset(planes[:].bitcast(I32), 0)
         nc.gpsimd.dma_start(out=bz_sb[:], in_=bz.rearrange("(p j) -> p j", j=PACK))
         nc.gpsimd.dma_start(out=bn_sb[:], in_=bn.rearrange("(p j) -> p j", j=PACK))
-        nc.gpsimd.tensor_scalar(out=bz_half[:], in0=bz_sb[:], scalar1=0.5, scalar2=0.0, op0=ALU.mult, op1=ALU.add)
+        nc.gpsimd.tensor_scalar(out=bz_neg[:], in0=bz_sb[:], scalar1=-1.0, scalar2=0.0, op0=ALU.mult, op1=ALU.add)
+
         for w in range(4):
             nc.sync.dma_start(out=stage[:, w * N // 4 : (w + 1) * N // 4], in_=w_scales[w][0].bitcast(I32))
         nc.sync.dma_start(out=stage[:, N:], in_=hq_scales[0].bitcast(I32))
         load_words(WZ)
-        load_words(UZ)
         load_rows(x_sb, x_rows, X_LOADS[0])
+        load_words(UZ)
+        load_words(UN)
         for r in range(4):
             nc.sync.dma_start(out=planes[r:P:32, :].bitcast(I32), in_=stage[r:16:4, :])
-        load_words(UN)
         load_hq(HQ_LOADS[0])
         load_words(WN)
         load_rows(x_sb, x_rows, X_LOADS[1])
-        load_rows(x_sb, x_rows, X_LOADS[2])
         load_rows(h_sb, h_rows, H_LOADS[0])
-        load_hq(HQ_LOADS[1])
-        load_rows(x_sb, x_rows, X_LOADS[3])
+        load_rows(x_sb, x_rows, X_LOADS[2])
         load_rows(h_sb, h_rows, H_LOADS[1])
+        load_hq(HQ_LOADS[1])
         load_rows(h_sb, h_rows, H_LOADS[2])
+        load_rows(x_sb, x_rows, X_LOADS[3])
+        load_rows(h_sb, h_rows, H_LOADS[3])
 
         round_x(0)
         round_x(1)
@@ -225,43 +246,52 @@ def tile_mix_gru_mgu_kernel(
         deal_words(UZ)
         quantize_x(0)
         deal_words(UN)
-        deal_scales(WZ, UN + 1)
-        product("sz", 0, [WZ, UZ], 2)
-        product("hn", 0, [UN], 3)
-        gate(0)
-        round_x(2)
+        for part in ((0, 2), (2, 2)):
+            deal_scales(WZ, UZ + 1, part[0], part[0] + part[1])
+            product("sz", 0, [WZ, UZ], 2, part)
+            gate(0, part)
         quantize_x(1)
+        deal_scales(UN, WN + 1)
+        product("hn", 0, [UN], 3)
+        product("sz", 1, [WZ, UZ], 2)
+        round_x(2)
+        gate(1)
+        product("hn", 1, [UN], 3)
         deal_words(WN)
-        deal_scales(WN, WN + 1)
 
-        for i in range(UNITS + 4):
-            if live(i + 1):
+        last = len(UNITS) - 1
+        for i in range(len(UNITS) + 5):
+            if live(i + 1) and i > 0:
                 product("sz", i + 1, [WZ, UZ], 2)
             if live(i):
                 product("xn", i, [WN], 3)
-            if live(i + 1):
+            if live(i + 1) and i > 0:
                 product("hn", i + 1, [UN], 3)
-            if live(i - 4):
-                round_out(i - 4, "vector" if i - 4 == UNITS - 1 else "scalar")
-            if live(i + 1):
+            if closes(i - 4) and i - 4 != last:
+                round_out(UNITS[i - 4][0])
+            if live(i + 1) and i > 0:
                 gate(i + 1)
-            if live(i - 2):
-                difference(i - 2)
+            if live(i) and i in POOL_UNITS:
+                kept_state(i)
             if live(i):
                 gated_state(i)
             if live(i - 1):
                 pre_activation(i - 1)
                 candidate(i - 1)
-            if live(i + 3):
-                round_x(i + 3)
-            if live(i + 2):
-                quantize_x(i + 2)
-            if live(i - 4):
-                hand_on(i - 4)
-            if live(i - 2):
-                step(i - 2)
+            if live(i) and i not in POOL_UNITS:
+                kept_state(i)
+            if opens(i + 3):
+                round_x(UNITS[i + 3][0])
+            if opens(i + 2):
+                quantize_x(UNITS[i + 2][0])
+            if i - 4 == last:
+                round_out(UNITS[last][0], "vector")
+            if closes(i - 5):
+                hand_on(UNITS[i - 5][0])
             if live(i - 3):
                 new_state(i - 3)
+            if live(i - 2):
+                gated_candidate(i - 2)
 
         for q in range(4):
             nc.sync.dma_start(out=scales_flat[4 * q : 4 * q + 4, :], in_=o_plane[32 * q : 32 * q + 4, :].bitcast(I32))

@@ -23,9 +23,9 @@ WZ, UZ, UN, WN = 0, 1, 2, 3
 WIDTHS = [128] * 8
 STARTS = [sum(WIDTHS[:c]) for c in range(len(WIDTHS) + 1)]
 UNITS = [(c, r0, BANK // w) for c, w in enumerate(WIDTHS) for r0 in range(0, PACK, BANK // w)]
-POOL_UNITS = tuple(range(8))
-X_LOADS = [(0, 2), (2, 3), (3, 5), (5, 8)]
-H_LOADS = [(0, 1), (1, 3), (3, 5), (5, 8)]
+POOL_UNITS = tuple(range(7))
+X_LOADS = [(0, 2), (2, 4), (4, 6), (6, 8)]
+H_LOADS = [(0, 2), (2, 4), (4, 6), (6, 8)]
 HQ_LOADS = [(0, 3), (3, 8)]
 CODE_STORES = [(0, 4), (4, 7), (7, 8)]
 KEPT_BUFS = 4
@@ -76,7 +76,7 @@ def tile_mix_gru_mgu_kernel(
         h_sb = {r: keep.tile([P, PACK, width(r)], F32, name="h%d" % r[0], align_bytes=64) for r in H_LOADS}
         hq_sb = {r: keep.tile([P, width(r)], I32, name="hq%d" % r[0], align_bytes=64) for r in HQ_LOADS}
         o_sb = [keep.tile([P, PACK, w], F32, name="o%d" % c, align_bytes=64) for c, w in enumerate(WIDTHS)]
-        x_bf = [keep.tile([P, PACK * w], BF16, name="xb%d" % c, align_bytes=64) for c, w in enumerate(WIDTHS)]
+        x_bf = [keep.tile([P, PACK * w], BF16, name="xb%d" % c, tag=("ring%d" % (c - 2) if 2 <= c < 5 else "xb%d" % c), align_bytes=64) for c, w in enumerate(WIDTHS)]
         o_bf = [keep.tile([P, PACK * w], BF16, name="ob%d" % c, align_bytes=64) for c, w in enumerate(WIDTHS)]
         x_code = keep.tile([P, T], U32, name="x_code", align_bytes=64)
         x_plane = keep.tile([P, T], U8, name="x_plane", align_bytes=64)
@@ -183,13 +183,15 @@ def tile_mix_gru_mgu_kernel(
 
         def kept_state(u):
             engine = nc.gpsimd if u in POOL_UNITS else nc.vector
-            engine.tensor_tensor(out=fresh("kept", u, KEPT_BUFS)[:], in0=tiles[("v", u)][:], in1=h_of(u), op=ALU.mult)
+            kept = keep.tile([P, PACK, WIDTHS[u]], F32, name="kept%d" % u, tag=("ring%d" % (u % 3) if u in POOL_UNITS else "kept_last"), align_bytes=64)
+            tiles[("kept", u)] = kept
+            engine.tensor_tensor(out=kept[:], in0=tiles[("v", u)][:], in1=h_of(u), op=ALU.mult)
 
         def gated_state(u):
             nc.vector.scalar_tensor_tensor(out=fresh("zh", u)[:], in0=tiles[("v", u)][:], scalar=1.0, in1=tiles[("hn", u)][:], op0=ALU.subtract, op1=ALU.mult)
 
         def pre_activation(u):
-            nc.vector.tensor_tensor(out=fresh("pre", u)[:], in0=tiles[("xn", u)][:], in1=tiles[("zh", u)][:], op=ALU.subtract)
+            nc.vector.scalar_tensor_tensor(out=fresh("pre", u)[:], in0=tiles[("zh", u)][:], scalar=-1.0, in1=tiles[("xn", u)][:], op0=ALU.mult, op1=ALU.add)
 
         def candidate(u):
             c, r0, rows = UNITS[u]
@@ -218,14 +220,13 @@ def tile_mix_gru_mgu_kernel(
         nc.vector.memset(planes[:].bitcast(I32), 0)
         nc.gpsimd.dma_start(out=bz_sb[:], in_=bz.rearrange("(p j) -> p j", j=PACK))
         nc.gpsimd.dma_start(out=bn_sb[:], in_=bn.rearrange("(p j) -> p j", j=PACK))
-        nc.gpsimd.tensor_scalar(out=bz_neg[:], in0=bz_sb[:], scalar1=-1.0, scalar2=0.0, op0=ALU.mult, op1=ALU.add)
 
         for w in range(4):
             nc.sync.dma_start(out=stage[:, w * N // 4 : (w + 1) * N // 4], in_=w_scales[w][0].bitcast(I32))
         nc.sync.dma_start(out=stage[:, N:], in_=hq_scales[0].bitcast(I32))
         load_words(WZ)
-        load_rows(x_sb, x_rows, X_LOADS[0])
         load_words(UZ)
+        load_rows(x_sb, x_rows, X_LOADS[0])
         load_words(UN)
         for r in range(4):
             nc.sync.dma_start(out=planes[r:P:32, :].bitcast(I32), in_=stage[r:16:4, :])
@@ -233,18 +234,19 @@ def tile_mix_gru_mgu_kernel(
         load_words(WN)
         load_rows(x_sb, x_rows, X_LOADS[1])
         load_rows(h_sb, h_rows, H_LOADS[0])
+        load_hq(HQ_LOADS[1])
         load_rows(x_sb, x_rows, X_LOADS[2])
         load_rows(h_sb, h_rows, H_LOADS[1])
-        load_hq(HQ_LOADS[1])
-        load_rows(h_sb, h_rows, H_LOADS[2])
         load_rows(x_sb, x_rows, X_LOADS[3])
+        load_rows(h_sb, h_rows, H_LOADS[2])
         load_rows(h_sb, h_rows, H_LOADS[3])
 
-        round_x(0)
-        round_x(1)
         deal_words(WZ)
         deal_words(UZ)
+        round_x(0, "vector")
+        round_x(1, "vector")
         quantize_x(0)
+        nc.vector.tensor_scalar(out=bz_neg[:], in0=bz_sb[:], scalar1=-1.0, scalar2=None, op0=ALU.mult)
         deal_words(UN)
         for part in ((0, 2), (2, 2)):
             deal_scales(WZ, UZ + 1, part[0], part[0] + part[1])
@@ -271,15 +273,13 @@ def tile_mix_gru_mgu_kernel(
                 round_out(UNITS[i - 4][0])
             if live(i + 1) and i > 0:
                 gate(i + 1)
-            if live(i) and i in POOL_UNITS:
-                kept_state(i)
+            if i - 1 in POOL_UNITS:
+                kept_state(i - 1)
             if live(i):
                 gated_state(i)
             if live(i - 1):
                 pre_activation(i - 1)
                 candidate(i - 1)
-            if live(i) and i not in POOL_UNITS:
-                kept_state(i)
             if opens(i + 3):
                 round_x(UNITS[i + 3][0])
             if opens(i + 2):
@@ -288,10 +288,13 @@ def tile_mix_gru_mgu_kernel(
                 round_out(UNITS[last][0], "vector")
             if closes(i - 5):
                 hand_on(UNITS[i - 5][0])
+            if live(i - 1) and i - 1 not in POOL_UNITS:
+                kept_state(i - 1)
             if live(i - 3):
                 new_state(i - 3)
             if live(i - 2):
                 gated_candidate(i - 2)
 
         for q in range(4):
-            nc.sync.dma_start(out=scales_flat[4 * q : 4 * q + 4, :], in_=o_plane[32 * q : 32 * q + 4, :].bitcast(I32))
+            queue = nc.sync if q % 2 == 0 else nc.scalar
+            queue.dma_start(out=scales_flat[4 * q : 4 * q + 4, :], in_=o_plane[32 * q : 32 * q + 4, :].bitcast(I32))

@@ -17,25 +17,15 @@ ACT = mybir.ActivationFunctionType
 
 P = 128
 PACK = 4
-BANK = 512
-SUM_N = 128
+BLOCKS = 16
 WZ, UZ, UN, WN = 0, 1, 2, 3
-WIDTHS = [128] * 8
-STARTS = [sum(WIDTHS[:c]) for c in range(len(WIDTHS) + 1)]
-UNITS = [(c, r0, BANK // w) for c, w in enumerate(WIDTHS) for r0 in range(0, PACK, BANK // w)]
-POOL_UNITS = tuple(range(7))
-X_LOADS = [(0, 2), (2, 4), (4, 6), (6, 8)]
-H_LOADS = [(0, 2), (2, 4), (4, 6), (6, 8)]
-HQ_LOADS = [(0, 3), (3, 8)]
-CODE_STORES = [(0, 4), (4, 7), (7, 8)]
-KEPT_BUFS = 4
 
-
-def find(ranges, c):
-    for lo, hi in ranges:
-        if lo <= c < hi:
-            return lo, hi
-    raise ValueError("chunk outside the ranges")
+W = 128
+UNITS = T // W
+LAST = UNITS - 1
+PAIR = 2
+HQ_FIRST = 3
+RING = 3
 
 
 def tile_mix_gru_mgu_kernel(
@@ -46,65 +36,62 @@ def tile_mix_gru_mgu_kernel(
     w_words = [wz_words, uz_words, un_words, wn_words]
     w_scales = [wz_scales, uz_scales, un_scales, wn_scales]
     x_rows = x.rearrange("(p j) t -> p j t", j=PACK)
-    h_rows = h.rearrange("(p j) t -> p j t", j=PACK)
-    out_rows = out_0.rearrange("(p j) t -> p j t", j=PACK)
-    hq_flat = hq_words[0].rearrange("p t i -> p (t i)").bitcast(I32)
-    codes_flat = out_1[0].rearrange("p t i -> p (t i)").bitcast(I32)
-    scales_flat = out_2[0].bitcast(I32)
+    h_rows = h.rearrange("(p r) t -> p r t", r=PACK)
+    out_rows = out_0.rearrange("(p r) t -> p r t", r=PACK)
+    hq_dram = hq_words[0].rearrange("p t i -> p (t i)").bitcast(I32)
+    codes_dram = out_1[0].rearrange("p t i -> p (t i)").bitcast(I32)
+    scales_dram = out_2[0].bitcast(I32)
 
     with ExitStack() as ctx:
         keep = ctx.enter_context(tc.tile_pool(name="keep", bufs=1))
-        work = ctx.enter_context(tc.tile_pool(name="work", bufs=len(UNITS)))
+        work = ctx.enter_context(tc.tile_pool(name="work", bufs=UNITS))
         psum = ctx.enter_context(tc.psum_pool(name="psum", bufs=1))
         ctx.enter_context(tc.manual_schedule())
 
-        def span(r):
-            return slice(STARTS[r[0]], STARTS[r[1]])
-
-        def width(r):
-            return STARTS[r[1]] - STARTS[r[0]]
-
-        def cols(c):
-            return span((c, c + 1))
-
-        stage = keep.tile([16, (4 * N + T) // 4], I32, name="stage")
+        hq_plane_at = 4 * N
+        staged = keep.tile([BLOCKS, (4 * N + T) // 4], I32, name="staged")
         planes = keep.tile([P, 4 * N + T], U8, name="planes", align_bytes=64)
         w_plane = keep.tile([P, 4 * N], U8, name="w_plane", align_bytes=64)
         w_raw = [keep.tile([P, 2 * N], U8, name="w_raw%d" % w, align_bytes=64) for w in range(4)]
         w_code = [keep.tile([P, 2 * N], U8, name="w_code%d" % w, align_bytes=64) for w in range(4)]
-        x_sb = {r: keep.tile([P, PACK, width(r)], F32, name="x%d" % r[0], align_bytes=64) for r in X_LOADS}
-        h_sb = {r: keep.tile([P, PACK, width(r)], F32, name="h%d" % r[0], align_bytes=64) for r in H_LOADS}
-        hq_sb = {r: keep.tile([P, width(r)], I32, name="hq%d" % r[0], align_bytes=64) for r in HQ_LOADS}
-        o_sb = [keep.tile([P, PACK, w], F32, name="o%d" % c, align_bytes=64) for c, w in enumerate(WIDTHS)]
-        x_bf = [keep.tile([P, PACK * w], BF16, name="xb%d" % c, tag=("ring%d" % (c - 2) if 2 <= c < 5 else "xb%d" % c), align_bytes=64) for c, w in enumerate(WIDTHS)]
-        o_bf = [keep.tile([P, PACK * w], BF16, name="ob%d" % c, align_bytes=64) for c, w in enumerate(WIDTHS)]
+        x_sb = [keep.tile([P, PACK, PAIR * W], F32, name="x%d" % i, align_bytes=64) for i in range(UNITS // PAIR)]
+        h_sb = [keep.tile([P, PACK, PAIR * W], F32, name="h%d" % i, align_bytes=64) for i in range(UNITS // PAIR)]
+        hq_first = keep.tile([P, HQ_FIRST * W], I32, name="hq_first", align_bytes=64)
+        hq_rest = keep.tile([P, T - HQ_FIRST * W], I32, name="hq_rest", align_bytes=64)
+        out_sb = [keep.tile([P, PACK, W], F32, name="out%d" % u, align_bytes=64) for u in range(UNITS)]
+        out_bf = [keep.tile([P, PACK * W], BF16, name="out_bf%d" % u, align_bytes=64) for u in range(UNITS)]
         x_code = keep.tile([P, T], U32, name="x_code", align_bytes=64)
         x_plane = keep.tile([P, T], U8, name="x_plane", align_bytes=64)
-        o_code = keep.tile([P, T], U32, name="o_code", align_bytes=64)
-        o_plane = keep.tile([P, T], U8, name="o_plane", align_bytes=64)
+        out_code = keep.tile([P, T], U32, name="out_code", align_bytes=64)
+        out_plane = keep.tile([P, T], U8, name="out_plane", align_bytes=64)
         bz_sb = keep.tile([P, PACK], F32, name="bz_sb")
         bz_neg = keep.tile([P, PACK], F32, name="bz_neg")
         bn_sb = keep.tile([P, PACK], F32, name="bn_sb")
 
+        def ring(u):
+            return "ring%d" % (u % RING)
+
+        x_bf = [
+            keep.tile(
+                [P, PACK * W], BF16, name="x_bf%d" % u, align_bytes=64,
+                tag=ring(u - 2) if 0 <= u - 2 < RING else "x_bf%d" % u,
+            )
+            for u in range(UNITS)
+        ]
+
         tiles = {}
 
-        def chunk_of(sb, ranges, c):
-            r = find(ranges, c)
-            return slice(STARTS[c] - STARTS[r[0]], STARTS[c + 1] - STARTS[r[0]]), sb[r]
+        def cols(first, last=None):
+            return slice(first * W, ((first if last is None else last) + 1) * W)
 
-        def h_of(u):
-            c, r0, rows = UNITS[u]
-            part, tile = chunk_of(h_sb, H_LOADS, c)
-            return tile[:, r0 : r0 + rows, part]
+        def unit_of(loads, u):
+            return loads[u // PAIR][:, :, cols(u % PAIR)]
 
-        def load_rows(sb, rows, r, queue=nc.sync):
-            queue.dma_start(out=sb[r][:], in_=rows[:, :, span(r)])
+        def load_pair(loads, rows, i):
+            nc.sync.dma_start(out=loads[i][:], in_=rows[:, :, cols(PAIR * i, PAIR * i + PAIR - 1)])
 
-        def load_hq(r):
-            nc.sync.dma_start(out=hq_sb[r][:], in_=hq_flat[:, span(r)])
-
-        def load_words(w, queue=nc.sync):
-            queue.dma_start(out=w_raw[w][:].bitcast(I32), in_=w_words[w][0].bitcast(I32))
+        def load_words(w):
+            nc.sync.dma_start(out=w_raw[w][:].bitcast(I32), in_=w_words[w][0].bitcast(I32))
 
         def deal_words(w):
             nc.vector.tensor_copy(
@@ -112,189 +99,193 @@ def tile_mix_gru_mgu_kernel(
                 in_=w_raw[w][:].rearrange("p (m r b) -> p r m b", r=PACK, b=2),
             )
 
-        def deal_scales(lo, hi, r0=0, r1=PACK):
+        def deal_scales(first, last, rows):
+            span = slice(first * N, (last + 1) * N)
             nc.vector.tensor_copy(
-                out=w_plane[:, lo * N : hi * N].rearrange("p (w r m) -> p w r m", r=PACK, m=P)[:, :, r0:r1, :],
-                in_=planes[:, lo * N : hi * N].rearrange("p (w m r) -> p w r m", r=PACK, m=P)[:, :, r0:r1, :],
+                out=w_plane[:, span].rearrange("p (w r m) -> p w r m", r=PACK, m=P)[:, :, rows, :],
+                in_=planes[:, span].rearrange("p (w m r) -> p w r m", r=PACK, m=P)[:, :, rows, :],
             )
 
-        def interleave(engine, dst, src):
-            out = dst[:].rearrange("p (c i j) -> p c j i", i=4, j=PACK)
-            in_ = src.rearrange("p j (c i) -> p c j i", i=4)
-            if engine == "scalar":
-                nc.scalar.copy(out=out, in_=in_)
-            else:
-                nc.vector.tensor_copy(out=out, in_=in_)
+        def round_to_words(copy, dst, src):
+            copy(
+                out=dst.rearrange("p (g i j) -> p g j i", i=4, j=PACK),
+                in_=src.rearrange("p j (g i) -> p g j i", i=4),
+            )
 
-        def round_x(c, engine="scalar"):
-            part, tile = chunk_of(x_sb, X_LOADS, c)
-            interleave(engine, x_bf[c], tile[:, :, part])
+        def round_x(u, copy):
+            round_to_words(copy, x_bf[u][:], unit_of(x_sb, u))
 
-        def round_out(c, engine="scalar"):
-            interleave(engine, o_bf[c], o_sb[c][:])
+        def round_out(u):
+            round_to_words(nc.scalar.copy, out_bf[u][:], out_sb[u][:])
 
-        def quantize_x(c):
-            nc.vector.quantize_mx(out=x_code[:, cols(c)].bitcast(FP8X4), scales=x_plane[:, cols(c)], in_=x_bf[c][:])
+        def quantize_x(u):
+            nc.vector.quantize_mx(out=x_code[:, cols(u)].bitcast(FP8X4), scales=x_plane[:, cols(u)], in_=x_bf[u][:])
 
-        def hand_on(c):
-            nc.vector.quantize_mx(out=o_code[:, cols(c)].bitcast(FP8X4), scales=o_plane[:, cols(c)], in_=o_bf[c][:])
-            r = find(CODE_STORES, c)
-            if c == r[1] - 1:
-                nc.sync.dma_start(out=codes_flat[:, span(r)], in_=o_code[:, span(r)].bitcast(I32))
+        def quantize_out(u):
+            nc.vector.quantize_mx(out=out_code[:, cols(u)].bitcast(FP8X4), scales=out_plane[:, cols(u)], in_=out_bf[u][:])
 
-        def product(key, u, weights, bufs, part=None):
-            c, r0, rows = UNITS[u]
-            if part is not None:
-                r0, rows = part
-            acc = psum.tile([P, rows, WIDTHS[c]], F32, name=key, bufs=bufs)
-            tiles[(key, u)] = acc
-            part, hq_tile = chunk_of(hq_sb, HQ_LOADS, c)
-            hq_code = hq_tile[:, part]
-            hq_plane = planes[:, 4 * N + STARTS[c] : 4 * N + STARTS[c + 1]]
-            n_pass = WIDTHS[c] if len(weights) == 1 or WIDTHS[c] == BANK else SUM_N
-            for r in range(r0, r0 + rows):
-                for t0 in range(0, WIDTHS[c], n_pass):
-                    ts = slice(t0, t0 + n_pass)
-                    for n, w in enumerate(weights):
-                        code, plane = (x_code[:, cols(c)], x_plane[:, cols(c)]) if w in (WZ, WN) else (hq_code, hq_plane)
-                        nc.tensor.matmul_mx(
-                            out=acc[:, r - r0, ts],
-                            lhsT=w_code[w][:, r * 2 * P : (r + 1) * 2 * P].bitcast(FP4X4),
-                            lhsT_scale=w_plane[:, w * N + r * P : w * N + (r + 1) * P],
-                            rhs=code[:, ts].bitcast(FP8X4),
-                            rhs_scale=plane[:, ts],
-                            start=(n == 0),
-                            stop=(n == len(weights) - 1),
-                        )
+        def store_codes(first, last):
+            nc.sync.dma_start(out=codes_dram[:, cols(first, last)], in_=out_code[:, cols(first, last)].bitcast(I32))
 
-        def fresh(key, u, bufs=len(UNITS)):
-            c, r0, rows = UNITS[u]
-            t = work.tile([P, rows, WIDTHS[c]], F32, name=key, align_bytes=64, bufs=bufs)
-            tiles[(key, u)] = t
-            return t
+        def product(name, u, weights, bufs, rows):
+            acc = psum.tile([P, len(rows), W], F32, name=name, bufs=bufs)
+            tiles[(name, u)] = acc
+            x_operand = (x_code[:, cols(u)], x_plane[:, cols(u)])
+            hq_operand = (
+                hq_first[:, cols(u)] if u < HQ_FIRST else hq_rest[:, cols(u - HQ_FIRST)],
+                planes[:, hq_plane_at + u * W : hq_plane_at + (u + 1) * W],
+            )
+            for slot, r in enumerate(rows):
+                for i, w in enumerate(weights):
+                    code, plane = x_operand if w in (WZ, WN) else hq_operand
+                    nc.tensor.matmul_mx(
+                        out=acc[:, slot, :],
+                        lhsT=w_code[w][:, r * 2 * P : (r + 1) * 2 * P].bitcast(FP4X4),
+                        lhsT_scale=w_plane[:, w * N + r * P : w * N + (r + 1) * P],
+                        rhs=code.bitcast(FP8X4),
+                        rhs_scale=plane,
+                        start=(i == 0),
+                        stop=(i == len(weights) - 1),
+                    )
 
-        def gate(u, part=None):
-            c, r0, rows = UNITS[u]
-            if part is not None:
-                r0, rows = part
-            v = fresh("v", u) if ("v", u) not in tiles else tiles[("v", u)]
-            for r in range(rows):
-                nc.scalar.activation(out=v[:, r0 - UNITS[u][1] + r, :], in_=tiles[("sz", u)][:, r, :], func=ACT.Sigmoid, bias=bz_neg[:, r0 + r : r0 + r + 1], scale=-1.0)
+        def gate_sum(u, rows=range(PACK)):
+            product("sz", u, [WZ, UZ], 2, rows)
 
-        def kept_state(u):
-            engine = nc.gpsimd if u in POOL_UNITS else nc.vector
-            kept = keep.tile([P, PACK, WIDTHS[u]], F32, name="kept%d" % u, tag=("ring%d" % (u % 3) if u in POOL_UNITS else "kept_last"), align_bytes=64)
+        def state_product(u):
+            product("hn", u, [UN], 3, range(PACK))
+
+        def input_product(u):
+            product("xn", u, [WN], 3, range(PACK))
+
+        def fresh(name, u):
+            tiles[(name, u)] = work.tile([P, PACK, W], F32, name=name, align_bytes=64)
+            return tiles[(name, u)]
+
+        def gate(u, v, rows=range(PACK)):
+            for slot, r in enumerate(rows):
+                nc.scalar.activation(
+                    out=v[:, r, :], in_=tiles[("sz", u)][:, slot, :], func=ACT.Sigmoid,
+                    bias=bz_neg[:, r : r + 1], scale=-1.0,
+                )
+
+        def kept_state(u, engine, tag):
+            kept = keep.tile([P, PACK, W], F32, name="kept%d" % u, tag=tag, align_bytes=64)
             tiles[("kept", u)] = kept
-            engine.tensor_tensor(out=kept[:], in0=tiles[("v", u)][:], in1=h_of(u), op=ALU.mult)
+            engine.tensor_tensor(out=kept[:], in0=tiles[("v", u)][:], in1=unit_of(h_sb, u), op=ALU.mult)
 
         def gated_state(u):
-            nc.vector.scalar_tensor_tensor(out=fresh("zh", u)[:], in0=tiles[("v", u)][:], scalar=1.0, in1=tiles[("hn", u)][:], op0=ALU.subtract, op1=ALU.mult)
-
-        def pre_activation(u):
-            nc.vector.scalar_tensor_tensor(out=fresh("pre", u)[:], in0=tiles[("zh", u)][:], scalar=-1.0, in1=tiles[("xn", u)][:], op0=ALU.mult, op1=ALU.add)
+            nc.vector.scalar_tensor_tensor(
+                out=fresh("zh", u)[:], in0=tiles[("v", u)][:], scalar=1.0, in1=tiles[("hn", u)][:],
+                op0=ALU.subtract, op1=ALU.mult,
+            )
 
         def candidate(u):
-            c, r0, rows = UNITS[u]
+            nc.vector.scalar_tensor_tensor(
+                out=fresh("pre", u)[:], in0=tiles[("zh", u)][:], scalar=-1.0, in1=tiles[("xn", u)][:],
+                op0=ALU.mult, op1=ALU.add,
+            )
             cand = fresh("cand", u)
-            for r in range(rows):
-                nc.scalar.activation(out=cand[:, r, :], in_=tiles[("pre", u)][:, r, :], func=ACT.Tanh, bias=bn_sb[:, r0 + r : r0 + r + 1])
+            for r in range(PACK):
+                nc.scalar.activation(
+                    out=cand[:, r, :], in_=tiles[("pre", u)][:, r, :], func=ACT.Tanh, bias=bn_sb[:, r : r + 1],
+                )
 
         def gated_candidate(u):
-            nc.vector.scalar_tensor_tensor(out=fresh("zc", u)[:], in0=tiles[("v", u)][:], scalar=1.0, in1=tiles[("cand", u)][:], op0=ALU.subtract, op1=ALU.mult)
+            nc.vector.scalar_tensor_tensor(
+                out=fresh("zc", u)[:], in0=tiles[("v", u)][:], scalar=1.0, in1=tiles[("cand", u)][:],
+                op0=ALU.subtract, op1=ALU.mult,
+            )
 
         def new_state(u):
-            c, r0, rows = UNITS[u]
-            nc.vector.tensor_tensor(out=o_sb[c][:, r0 : r0 + rows, :], in0=tiles[("kept", u)][:], in1=tiles[("zc", u)][:], op=ALU.subtract)
-            if r0 + rows == PACK:
-                nc.sync.dma_start(out=out_rows[:, :, cols(c)], in_=o_sb[c][:])
-
-        def live(u):
-            return 0 <= u < len(UNITS)
-
-        def opens(u):
-            return live(u) and UNITS[u][1] == 0
-
-        def closes(u):
-            return live(u) and UNITS[u][1] + UNITS[u][2] == PACK
+            nc.vector.tensor_tensor(out=out_sb[u][:], in0=tiles[("kept", u)][:], in1=tiles[("zc", u)][:], op=ALU.subtract)
+            nc.sync.dma_start(out=out_rows[:, :, cols(u)], in_=out_sb[u][:])
 
         nc.vector.memset(planes[:].bitcast(I32), 0)
-        nc.gpsimd.dma_start(out=bz_sb[:], in_=bz.rearrange("(p j) -> p j", j=PACK))
-        nc.gpsimd.dma_start(out=bn_sb[:], in_=bn.rearrange("(p j) -> p j", j=PACK))
-
+        nc.gpsimd.dma_start(out=bz_sb[:], in_=bz.rearrange("(p r) -> p r", r=PACK))
+        nc.gpsimd.dma_start(out=bn_sb[:], in_=bn.rearrange("(p r) -> p r", r=PACK))
         for w in range(4):
-            nc.sync.dma_start(out=stage[:, w * N // 4 : (w + 1) * N // 4], in_=w_scales[w][0].bitcast(I32))
-        nc.sync.dma_start(out=stage[:, N:], in_=hq_scales[0].bitcast(I32))
+            nc.sync.dma_start(out=staged[:, w * N // 4 : (w + 1) * N // 4], in_=w_scales[w][0].bitcast(I32))
+        nc.sync.dma_start(out=staged[:, hq_plane_at // 4 :], in_=hq_scales[0].bitcast(I32))
         load_words(WZ)
         load_words(UZ)
-        load_rows(x_sb, x_rows, X_LOADS[0])
+        load_pair(x_sb, x_rows, 0)
         load_words(UN)
-        for r in range(4):
-            nc.sync.dma_start(out=planes[r:P:32, :].bitcast(I32), in_=stage[r:16:4, :])
-        load_hq(HQ_LOADS[0])
+        for i in range(4):
+            nc.sync.dma_start(out=planes[i:P:32, :].bitcast(I32), in_=staged[i:BLOCKS:4, :])
+        nc.sync.dma_start(out=hq_first[:], in_=hq_dram[:, cols(0, HQ_FIRST - 1)])
         load_words(WN)
-        load_rows(x_sb, x_rows, X_LOADS[1])
-        load_rows(h_sb, h_rows, H_LOADS[0])
-        load_hq(HQ_LOADS[1])
-        load_rows(x_sb, x_rows, X_LOADS[2])
-        load_rows(h_sb, h_rows, H_LOADS[1])
-        load_rows(x_sb, x_rows, X_LOADS[3])
-        load_rows(h_sb, h_rows, H_LOADS[2])
-        load_rows(h_sb, h_rows, H_LOADS[3])
+        for i in range(UNITS // PAIR):
+            if i + 1 < UNITS // PAIR:
+                load_pair(x_sb, x_rows, i + 1)
+            load_pair(h_sb, h_rows, i)
+            if i == 0:
+                nc.sync.dma_start(out=hq_rest[:], in_=hq_dram[:, cols(HQ_FIRST, LAST)])
 
         deal_words(WZ)
         deal_words(UZ)
-        round_x(0, "vector")
-        round_x(1, "vector")
+        round_x(0, nc.vector.tensor_copy)
+        round_x(1, nc.vector.tensor_copy)
         quantize_x(0)
         nc.vector.tensor_scalar(out=bz_neg[:], in0=bz_sb[:], scalar1=-1.0, scalar2=None, op0=ALU.mult)
         deal_words(UN)
-        for part in ((0, 2), (2, 2)):
-            deal_scales(WZ, UZ + 1, part[0], part[0] + part[1])
-            product("sz", 0, [WZ, UZ], 2, part)
-            gate(0, part)
+        v_first = fresh("v", 0)
+        for r0 in range(0, PACK, PACK // 2):
+            deal_scales(WZ, UZ, slice(r0, r0 + PACK // 2))
+            gate_sum(0, range(r0, r0 + PACK // 2))
+            gate(0, v_first, range(r0, r0 + PACK // 2))
         quantize_x(1)
-        deal_scales(UN, WN + 1)
-        product("hn", 0, [UN], 3)
-        product("sz", 1, [WZ, UZ], 2)
-        round_x(2)
-        gate(1)
-        product("hn", 1, [UN], 3)
+        deal_scales(UN, WN, slice(0, PACK))
+        state_product(0)
+        gate_sum(1)
+        round_x(2, nc.scalar.copy)
+        gate(1, fresh("v", 1))
+        state_product(1)
         deal_words(WN)
 
-        last = len(UNITS) - 1
-        for i in range(len(UNITS) + 5):
-            if live(i + 1) and i > 0:
-                product("sz", i + 1, [WZ, UZ], 2)
-            if live(i):
-                product("xn", i, [WN], 3)
-            if live(i + 1) and i > 0:
-                product("hn", i + 1, [UN], 3)
-            if closes(i - 4) and i - 4 != last:
-                round_out(UNITS[i - 4][0])
-            if live(i + 1) and i > 0:
-                gate(i + 1)
-            if i - 1 in POOL_UNITS:
-                kept_state(i - 1)
-            if live(i):
-                gated_state(i)
-            if live(i - 1):
-                pre_activation(i - 1)
+        for i in range(UNITS):
+            look_ahead = 0 < i < LAST
+            if look_ahead:
+                gate_sum(i + 1)
+            input_product(i)
+            if look_ahead:
+                state_product(i + 1)
+            if i >= 4:
+                round_out(i - 4)
+            if look_ahead:
+                gate(i + 1, fresh("v", i + 1))
+            if i >= 1:
+                kept_state(i - 1, nc.gpsimd, ring(i - 1))
+            gated_state(i)
+            if i >= 1:
                 candidate(i - 1)
-            if opens(i + 3):
-                round_x(UNITS[i + 3][0])
-            if opens(i + 2):
-                quantize_x(UNITS[i + 2][0])
-            if i - 4 == last:
-                round_out(UNITS[last][0], "vector")
-            if closes(i - 5):
-                hand_on(UNITS[i - 5][0])
-            if live(i - 1) and i - 1 not in POOL_UNITS:
-                kept_state(i - 1)
-            if live(i - 3):
+            if i + 3 <= LAST:
+                round_x(i + 3, nc.scalar.copy)
+            if i + 2 <= LAST:
+                quantize_x(i + 2)
+            if i >= 5:
+                quantize_out(i - 5)
+            if i >= 3:
                 new_state(i - 3)
-            if live(i - 2):
+            if i >= 2:
                 gated_candidate(i - 2)
 
+        round_out(LAST - 3)
+        candidate(LAST)
+        quantize_out(LAST - 4)
+        store_codes(0, LAST - 4)
+        kept_state(LAST, nc.vector, "kept_last")
+        new_state(LAST - 2)
+        round_out(LAST - 2)
+        gated_candidate(LAST - 1)
+        gated_candidate(LAST)
+        for u in (LAST - 1, LAST):
+            new_state(u)
+            round_out(u)
+        for u in range(LAST - 3, LAST):
+            quantize_out(u)
+        store_codes(LAST - 3, LAST - 1)
+        quantize_out(LAST)
+        store_codes(LAST, LAST)
         for q in range(4):
             queue = nc.sync if q % 2 == 0 else nc.scalar
-            queue.dma_start(out=scales_flat[4 * q : 4 * q + 4, :], in_=o_plane[32 * q : 32 * q + 4, :].bitcast(I32))
+            queue.dma_start(out=scales_dram[4 * q : 4 * q + 4, :], in_=out_plane[32 * q : 32 * q + 4, :].bitcast(I32))

from contextlib import ExitStack

import concourse.mybir as mybir

K, N, T = 512, 512, 1024
FLOPS = 4 * 2 * K * N * T

F32 = mybir.dt.float32
BF16 = mybir.dt.bfloat16
I32 = mybir.dt.int32
U32 = mybir.dt.uint32
U8 = mybir.dt.uint8
FP8X4 = mybir.dt.float8_e4m3fn_x4
FP4X4 = mybir.dt.float4_e2m1fn_x4
ALU = mybir.AluOpType
ACT = mybir.ActivationFunctionType

P = 128
PACK = 4
BLOCKS = 16
WZ, UZ, UN, WN = 0, 1, 2, 3

W = 128
UNITS = T // W
LAST = UNITS - 1
PAIR = 2
HQ_FIRST = 3
RING = 3


def tile_mix_gru_mgu_kernel(
    tc, x, hq_words, hq_scales, wz_words, wz_scales, uz_words, uz_scales,
    wn_words, wn_scales, un_words, un_scales, bz, bn, h, out_0, out_1, out_2,
):
    nc = tc.nc
    w_words = [wz_words, uz_words, un_words, wn_words]
    w_scales = [wz_scales, uz_scales, un_scales, wn_scales]
    x_rows = x.rearrange("(p j) t -> p j t", j=PACK)
    h_rows = h.rearrange("(p r) t -> p r t", r=PACK)
    out_rows = out_0.rearrange("(p r) t -> p r t", r=PACK)
    hq_dram = hq_words[0].rearrange("p t i -> p (t i)").bitcast(I32)
    codes_dram = out_1[0].rearrange("p t i -> p (t i)").bitcast(I32)
    scales_dram = out_2[0].bitcast(I32)

    with ExitStack() as ctx:
        keep = ctx.enter_context(tc.tile_pool(name="keep", bufs=1))
        work = ctx.enter_context(tc.tile_pool(name="work", bufs=UNITS))
        psum = ctx.enter_context(tc.psum_pool(name="psum", bufs=1))
        ctx.enter_context(tc.manual_schedule())

        hq_plane_at = 4 * N
        staged = keep.tile([BLOCKS, (4 * N + T) // 4], I32, name="staged")
        planes = keep.tile([P, 4 * N + T], U8, name="planes", align_bytes=64)
        w_plane = keep.tile([P, 4 * N], U8, name="w_plane", align_bytes=64)
        w_raw = [keep.tile([P, 2 * N], U8, name="w_raw%d" % w, align_bytes=64) for w in range(4)]
        w_code = [keep.tile([P, 2 * N], U8, name="w_code%d" % w, align_bytes=64) for w in range(4)]
        x_sb = [keep.tile([P, PACK, PAIR * W], F32, name="x%d" % i, align_bytes=64) for i in range(UNITS // PAIR)]
        h_sb = [keep.tile([P, PACK, PAIR * W], F32, name="h%d" % i, align_bytes=64) for i in range(UNITS // PAIR)]
        hq_first = keep.tile([P, HQ_FIRST * W], I32, name="hq_first", align_bytes=64)
        hq_rest = keep.tile([P, T - HQ_FIRST * W], I32, name="hq_rest", align_bytes=64)
        out_sb = [keep.tile([P, PACK, W], F32, name="out%d" % u, align_bytes=64) for u in range(UNITS)]
        out_bf = [keep.tile([P, PACK * W], BF16, name="out_bf%d" % u, align_bytes=64) for u in range(UNITS)]
        x_code = keep.tile([P, T], U32, name="x_code", align_bytes=64)
        x_plane = keep.tile([P, T], U8, name="x_plane", align_bytes=64)
        out_code = keep.tile([P, T], U32, name="out_code", align_bytes=64)
        out_plane = keep.tile([P, T], U8, name="out_plane", align_bytes=64)
        bz_sb = keep.tile([P, PACK], F32, name="bz_sb")
        bz_neg = keep.tile([P, PACK], F32, name="bz_neg")
        bn_sb = keep.tile([P, PACK], F32, name="bn_sb")

        def ring(u):
            return "ring%d" % (u % RING)

        x_bf = [
            keep.tile(
                [P, PACK * W], BF16, name="x_bf%d" % u, align_bytes=64,
                tag=ring(u - 2) if 0 <= u - 2 < RING else "x_bf%d" % u,
            )
            for u in range(UNITS)
        ]

        tiles = {}

        def cols(first, last=None):
            return slice(first * W, ((first if last is None else last) + 1) * W)

        def unit_of(loads, u):
            return loads[u // PAIR][:, :, cols(u % PAIR)]

        def load_pair(loads, rows, i):
            nc.sync.dma_start(out=loads[i][:], in_=rows[:, :, cols(PAIR * i, PAIR * i + PAIR - 1)])

        def load_words(w):
            nc.sync.dma_start(out=w_raw[w][:].bitcast(I32), in_=w_words[w][0].bitcast(I32))

        def deal_words(w):
            nc.vector.tensor_copy(
                out=w_code[w][:].rearrange("p (r m b) -> p r m b", r=PACK, b=2),
                in_=w_raw[w][:].rearrange("p (m r b) -> p r m b", r=PACK, b=2),
            )

        def deal_scales(first, last, rows):
            span = slice(first * N, (last + 1) * N)
            nc.vector.tensor_copy(
                out=w_plane[:, span].rearrange("p (w r m) -> p w r m", r=PACK, m=P)[:, :, rows, :],
                in_=planes[:, span].rearrange("p (w m r) -> p w r m", r=PACK, m=P)[:, :, rows, :],
            )

        def round_to_words(copy, dst, src):
            copy(
                out=dst.rearrange("p (g i j) -> p g j i", i=4, j=PACK),
                in_=src.rearrange("p j (g i) -> p g j i", i=4),
            )

        def round_x(u, copy):
            round_to_words(copy, x_bf[u][:], unit_of(x_sb, u))

        def round_out(u):
            round_to_words(nc.scalar.copy, out_bf[u][:], out_sb[u][:])

        def quantize_x(u):
            nc.vector.quantize_mx(out=x_code[:, cols(u)].bitcast(FP8X4), scales=x_plane[:, cols(u)], in_=x_bf[u][:])

        def quantize_out(u):
            nc.vector.quantize_mx(out=out_code[:, cols(u)].bitcast(FP8X4), scales=out_plane[:, cols(u)], in_=out_bf[u][:])

        def store_codes(first, last):
            nc.sync.dma_start(out=codes_dram[:, cols(first, last)], in_=out_code[:, cols(first, last)].bitcast(I32))

        def product(name, u, weights, bufs, rows):
            acc = psum.tile([P, len(rows), W], F32, name=name, bufs=bufs)
            tiles[(name, u)] = acc
            x_operand = (x_code[:, cols(u)], x_plane[:, cols(u)])
            hq_operand = (
                hq_first[:, cols(u)] if u < HQ_FIRST else hq_rest[:, cols(u - HQ_FIRST)],
                planes[:, hq_plane_at + u * W : hq_plane_at + (u + 1) * W],
            )
            for slot, r in enumerate(rows):
                for i, w in enumerate(weights):
                    code, plane = x_operand if w in (WZ, WN) else hq_operand
                    nc.tensor.matmul_mx(
                        out=acc[:, slot, :],
                        lhsT=w_code[w][:, r * 2 * P : (r + 1) * 2 * P].bitcast(FP4X4),
                        lhsT_scale=w_plane[:, w * N + r * P : w * N + (r + 1) * P],
                        rhs=code.bitcast(FP8X4),
                        rhs_scale=plane,
                        start=(i == 0),
                        stop=(i == len(weights) - 1),
                    )

        def gate_sum(u, rows=range(PACK)):
            product("sz", u, [WZ, UZ], 2, rows)

        def state_product(u):
            product("hn", u, [UN], 3, range(PACK))

        def input_product(u):
            product("xn", u, [WN], 3, range(PACK))

        def fresh(name, u):
            tiles[(name, u)] = work.tile([P, PACK, W], F32, name=name, align_bytes=64)
            return tiles[(name, u)]

        def gate(u, v, rows=range(PACK)):
            for slot, r in enumerate(rows):
                nc.scalar.activation(
                    out=v[:, r, :], in_=tiles[("sz", u)][:, slot, :], func=ACT.Sigmoid,
                    bias=bz_neg[:, r : r + 1], scale=-1.0,
                )

        def kept_state(u, engine, tag):
            kept = keep.tile([P, PACK, W], F32, name="kept%d" % u, tag=tag, align_bytes=64)
            tiles[("kept", u)] = kept
            engine.tensor_tensor(out=kept[:], in0=tiles[("v", u)][:], in1=unit_of(h_sb, u), op=ALU.mult)

        def gated_state(u):
            nc.vector.scalar_tensor_tensor(
                out=fresh("zh", u)[:], in0=tiles[("v", u)][:], scalar=1.0, in1=tiles[("hn", u)][:],
                op0=ALU.subtract, op1=ALU.mult,
            )

        def candidate(u):
            nc.vector.scalar_tensor_tensor(
                out=fresh("pre", u)[:], in0=tiles[("zh", u)][:], scalar=-1.0, in1=tiles[("xn", u)][:],
                op0=ALU.mult, op1=ALU.add,
            )
            cand = fresh("cand", u)
            for r in range(PACK):
                nc.scalar.activation(
                    out=cand[:, r, :], in_=tiles[("pre", u)][:, r, :], func=ACT.Tanh, bias=bn_sb[:, r : r + 1],
                )

        def gated_candidate(u):
            nc.vector.scalar_tensor_tensor(
                out=fresh("zc", u)[:], in0=tiles[("v", u)][:], scalar=1.0, in1=tiles[("cand", u)][:],
                op0=ALU.subtract, op1=ALU.mult,
            )

        def new_state(u):
            nc.vector.tensor_tensor(out=out_sb[u][:], in0=tiles[("kept", u)][:], in1=tiles[("zc", u)][:], op=ALU.subtract)
            nc.sync.dma_start(out=out_rows[:, :, cols(u)], in_=out_sb[u][:])

        nc.vector.memset(planes[:].bitcast(I32), 0)
        nc.gpsimd.dma_start(out=bz_sb[:], in_=bz.rearrange("(p r) -> p r", r=PACK))
        nc.gpsimd.dma_start(out=bn_sb[:], in_=bn.rearrange("(p r) -> p r", r=PACK))
        for w in range(4):
            nc.sync.dma_start(out=staged[:, w * N // 4 : (w + 1) * N // 4], in_=w_scales[w][0].bitcast(I32))
        nc.sync.dma_start(out=staged[:, hq_plane_at // 4 :], in_=hq_scales[0].bitcast(I32))
        load_words(WZ)
        load_words(UZ)
        load_pair(x_sb, x_rows, 0)
        load_words(UN)
        for i in range(4):
            nc.sync.dma_start(out=planes[i:P:32, :].bitcast(I32), in_=staged[i:BLOCKS:4, :])
        nc.sync.dma_start(out=hq_first[:], in_=hq_dram[:, cols(0, HQ_FIRST - 1)])
        load_words(WN)
        for i in range(UNITS // PAIR):
            if i + 1 < UNITS // PAIR:
                load_pair(x_sb, x_rows, i + 1)
            load_pair(h_sb, h_rows, i)
            if i == 0:
                nc.sync.dma_start(out=hq_rest[:], in_=hq_dram[:, cols(HQ_FIRST, LAST)])

        deal_words(WZ)
        deal_words(UZ)
        round_x(0, nc.vector.tensor_copy)
        round_x(1, nc.vector.tensor_copy)
        quantize_x(0)
        nc.vector.tensor_scalar(out=bz_neg[:], in0=bz_sb[:], scalar1=-1.0, scalar2=None, op0=ALU.mult)
        deal_words(UN)
        v_first = fresh("v", 0)
        for r0 in range(0, PACK, PACK // 2):
            deal_scales(WZ, UZ, slice(r0, r0 + PACK // 2))
            gate_sum(0, range(r0, r0 + PACK // 2))
            gate(0, v_first, range(r0, r0 + PACK // 2))
        quantize_x(1)
        deal_scales(UN, WN, slice(0, PACK))
        state_product(0)
        gate_sum(1)
        round_x(2, nc.scalar.copy)
        gate(1, fresh("v", 1))
        state_product(1)
        deal_words(WN)

        for i in range(UNITS):
            look_ahead = 0 < i < LAST
            if look_ahead:
                gate_sum(i + 1)
            input_product(i)
            if look_ahead:
                state_product(i + 1)
            if i >= 4:
                round_out(i - 4)
            if look_ahead:
                gate(i + 1, fresh("v", i + 1))
            if i >= 1:
                kept_state(i - 1, nc.gpsimd, ring(i - 1))
            gated_state(i)
            if i >= 1:
                candidate(i - 1)
            if i + 3 <= LAST:
                round_x(i + 3, nc.scalar.copy)
            if i + 2 <= LAST:
                quantize_x(i + 2)
            if i >= 5:
                quantize_out(i - 5)
            if i >= 3:
                new_state(i - 3)
            if i >= 2:
                gated_candidate(i - 2)

        round_out(LAST - 3)
        candidate(LAST)
        quantize_out(LAST - 4)
        store_codes(0, LAST - 4)
        kept_state(LAST, nc.vector, "kept_last")
        new_state(LAST - 2)
        round_out(LAST - 2)
        gated_candidate(LAST - 1)
        gated_candidate(LAST)
        for u in (LAST - 1, LAST):
            new_state(u)
            round_out(u)
        for u in range(LAST - 3, LAST):
            quantize_out(u)
        store_codes(LAST - 3, LAST - 1)
        quantize_out(LAST)
        store_codes(LAST, LAST)
        for q in range(4):
            queue = nc.sync if q % 2 == 0 else nc.scalar
            queue.dma_start(out=scales_dram[4 * q : 4 * q + 4, :], in_=out_plane[32 * q : 32 * q + 4, :].bitcast(I32))
